import numpy as np
import ml_dtypes


def mxq(x, axis, fmt="e4m3"):
    dtype, down = {"e4m3": (ml_dtypes.float8_e4m3fn, 7), "e5m2": (ml_dtypes.float8_e5m2, 14)}[fmt]
    v = np.moveaxis(np.asarray(x, np.float32).astype(ml_dtypes.bfloat16).astype(np.float64), axis, -1)
    blocks = v.reshape(v.shape[:-1] + (-1, 32))
    amax = np.abs(blocks).max(-1, keepdims=True)
    byte = np.maximum(np.where(amax > 0, np.frexp(amax)[1] - 1 + 127, 0) - down, 1)
    scale = np.exp2(byte - 127.0)
    codes = (blocks / scale).astype(np.float32).astype(dtype).astype(np.float64)
    return np.moveaxis((codes * scale).reshape(v.shape), -1, axis)


WIDE = False


def mx_kscale(k):
    if not WIDE:
        return np.ones(k)
    levels = np.array([10, -10, 5, -5, 0])
    if k % 512:
        return np.exp2(np.random.permutation(np.resize(levels, k // 32))).repeat(32)
    a = np.empty((k // 512, 16))
    for p in range(k // 512):
        a[p, :8] = np.random.permutation(np.resize(levels, 8))
        for g in range(8):
            far = levels[np.abs(levels - a[p, g]) >= 10]
            a[p, g + 8] = far[np.random.randint(len(far))]
    return np.exp2(a.ravel()).repeat(32)


def f64(x):
    return np.asarray(x).astype(np.float64)


def striped(idx):
    return np.tile(idx.reshape(-1, 16).T, (8, 1)).astype(np.uint16)


def unstriped(offs):
    return offs[:16].T.reshape(-1).astype(np.int64)


def striped8(idx):
    return np.concatenate([x.reshape(-1, 16).T for x in idx]).astype(np.uint16)


def runs(offs, k):
    lists = np.stack([offs[16 * r : 16 * r + 16].T.reshape(-1) for r in range(8)]).astype(np.int64)
    return lists[np.arange(k) % 512 // 64]


def pack_weight(w):
    k, n = w.shape
    w = f64(np.asarray(w, np.float32).astype(ml_dtypes.bfloat16)).reshape(k // 32, 32, n)
    amax = np.abs(w).max(1)
    byte = np.clip(np.where(amax > 0, np.frexp(amax)[1] - 1 + 127 - 7, 1), 1, 254)
    scaled = (w * np.exp2(127.0 - byte)[:, None, :]).reshape(k, n).astype(np.float32)
    words = np.ascontiguousarray(scaled.reshape(k // 512, 128, 4, n).transpose(0, 1, 3, 2)).astype(ml_dtypes.float8_e4m3fn).view(np.uint8)
    return words, np.ascontiguousarray(byte.astype(np.uint8).reshape(k // 512, 16, n))


def unpack_weight(words, scales):
    g, p, n, _ = words.shape
    vals = np.ascontiguousarray(words).view(ml_dtypes.float8_e4m3fn).astype(np.float64) * np.repeat(np.exp2(scales.astype(np.float64) - 127.0), 8, axis=1)[..., None]
    return vals.transpose(0, 1, 3, 2).reshape(g * 512, n)

def planes(y):
    n, m = y.shape
    v = y.astype(np.float32).astype(ml_dtypes.bfloat16).astype(np.float64).reshape(n // 32, 32, m)
    top = np.abs(v).max(1)
    byte = np.clip(np.where(top > 0, np.frexp(top)[1] - 1 + 127 - 7, 1), 1, 254)
    codes = (v * np.exp2(127.0 - byte)[:, None, :]).reshape(n, m).astype(np.float32).astype(ml_dtypes.float8_e4m3fn).view(np.uint8)
    words = codes.reshape(n // 512, 128, 4, m).transpose(0, 1, 3, 2)
    return np.ascontiguousarray(words), np.ascontiguousarray(byte.astype(np.uint8).reshape(n // 512, 16, m))


K, T, S, V, N, H = 512, 2048, 512, 256, 512, 512


def setup_inputs():
    n = np.random.standard_normal
    s = mx_kscale(K)[:, None]
    u = mx_kscale(H)
    packed_xT = pack_weight(n((K, T)) * s)
    packed_w1 = pack_weight(n((K, H)) / np.sqrt(K) / s)
    packed_w2 = pack_weight(n((H, N)) / np.sqrt(2 * H) / u[:, None])
    packed_w3 = pack_weight(n((K, N)) / np.sqrt(2 * K) / s)
    return {
        "x_words": packed_xT[0],
        "x_scales": packed_xT[1],
        "w1_words": packed_w1[0],
        "w1_scales": packed_w1[1],
        "gn": (np.random.uniform(0.5, 1.5, (H, 1)) * u[:, None]).astype(np.float32),
        "w2_words": packed_w2[0],
        "w2_scales": packed_w2[1],
        "w3_words": packed_w3[0],
        "w3_scales": packed_w3[1],
        "offs": striped8(np.random.randint(0, T, (8, S))),
        "n1": striped8(np.stack([np.random.permutation(S) for _ in range(8)])),
        "two": striped(np.random.permutation(T)[:V]),
        "n2": striped(np.random.permutation(V)),
        "n3": striped(np.random.permutation(V)),
    }


def reference(x_words, x_scales, w1_words, w1_scales, gn, w2_words, w2_scales, w3_words, w3_scales, offs, n1, two, n2, n3):
    xq = unpack_weight(x_words, x_scales)[np.arange(K)[:, None], runs(offs, K)]
    y = unpack_weight(w1_words, w1_scales).T @ xq
    ln = y[np.arange(H)[:, None], runs(n1, H)]
    sq = (ln) ** 2
    ms = sq.reshape(H, V, 2).sum(axis=2)
    z = f64(gn) * np.sqrt(ms + 0.1)
    x_two = unpack_weight(x_words, x_scales)[:, unstriped(two)]
    h = unpack_weight(w2_words, w2_scales).T @ mxq(z, 0, "e4m3") + unpack_weight(w3_words, w3_scales).T @ x_two
    out_0 = h[:, unstriped(n2)] * h[:, unstriped(n3)]
    return (out_0,) + planes(out_0)

@@ -1,0 +1,237 @@
+from contextlib import ExitStack
+
+import concourse.mybir as mybir
+
+K, T, S, V, N, H = 512, 2048, 512, 256, 512, 512
+FLOPS = 2 * K * H * S + 2 * H * N * V + 2 * K * N * V
+
+F32 = mybir.dt.float32
+BF16 = mybir.dt.bfloat16
+I32 = mybir.dt.int32
+U32 = mybir.dt.uint32
+U16 = mybir.dt.uint16
+U8 = mybir.dt.uint8
+FP8X4 = mybir.dt.float8_e4m3fn_x4
+ACT = mybir.ActivationFunctionType
+ALU = mybir.AluOpType
+
+P = 128
+PACK = 4
+QUAD = 32
+HALF = S // 2
+VH = V // 2
+SPARE = 16
+
+
+def tile_picked_hmixhprmsprod_none_po_kernel(
+    tc, x_words, x_scales, w1_words, w1_scales, gn, w2_words, w2_scales, w3_words, w3_scales,
+    offs, n1, two, n2, n3, out_0, out_1, out_2,
+):
+    nc = tc.nc
+
+    def hbm_words(words):
+        return words[0].rearrange("p c r -> p (c r)").bitcast(I32)
+
+    with ExitStack() as ctx:
+        lists = ctx.enter_context(tc.tile_pool(name="lists", bufs=1))
+        sb = ctx.enter_context(tc.tile_pool(name="sb", bufs=1))
+        ps = ctx.enter_context(tc.psum_pool(name="ps", bufs=1))
+
+        def sbt(name, shape, dtype):
+            return sb.tile(shape, dtype, name=name, align_bytes=64)
+
+        offs_t = lists.tile([P, S // 16], U16, name="offs_t")
+        n1_t = lists.tile([P, S // 16], U16, name="n1_t")
+        two_t = lists.tile([P, V // 16], U16, name="two_t")
+        n2_t = lists.tile([P, V // 16], U16, name="n2_t")
+        n3_t = lists.tile([P, V // 16], U16, name="n3_t")
+
+        xw = sbt("xw", [P, T], I32)
+        xs = sbt("xs", [P, T], U8)
+        w_raw = [sbt("w_raw%d" % i, [P, N], I32) for i in range(3)]
+        w_deal = [sbt("w_deal%d" % i, [P, N], I32) for i in range(3)]
+        ws_raw = sbt("ws_raw", [P, N], U8)
+        w1s = sbt("w1s", [P, N], U8)
+        w23s = sbt("w23s", [P, N], U8)
+        gain = sbt("gain", [P, 1, PACK], F32)
+        pick_w = sbt("pick_w", [P, S], U32)
+        pick_s = sbt("pick_s", [P, S], U8)
+        pick_plane = sbt("pick_plane", [P, S], U8)
+        two_w = sbt("two_w", [P, V], U32)
+        two_s = sbt("two_s", [P, V], U8)
+        hwin = [sbt("hwin%d" % t, [P, V + SPARE], F32) for t in range(PACK)]
+
+        xs_rows = x_scales[0].bitcast(I32)
+        xs_i = xs[:].bitcast(I32)
+
+        nc.vector.memset(xs_i, 0)
+        nc.vector.memset(ws_raw[:].bitcast(I32), 0)
+        nc.gpsimd.dma_start(xw[:], hbm_words(x_words))
+        nc.sync.dma_start(offs_t[:], offs)
+        nc.scalar.dma_start(xs_i[0:P:16, :], xs_rows[0:16:2, :])
+        nc.scalar.dma_start(xs_i[1:P:16, :], xs_rows[1:16:2, :])
+        nc.sync.dma_start(two_t[:], two)
+        nc.sync.dma_start(n1_t[:], n1)
+        nc.sync.dma_start(n2_t[:], n2)
+        nc.sync.dma_start(n3_t[:], n3)
+        nc.sync.dma_start(w_raw[0][:], hbm_words(w1_words))
+
+        def load_scale_rows(queue, scales, k):
+            rows = scales[0].bitcast(I32)
+            dst = ws_raw[:].bitcast(I32)
+            for q in range(4):
+                queue.dma_start(dst[QUAD * q + k : QUAD * q + k + 4, :], rows[4 * q : 4 * q + 4, :])
+
+        load_scale_rows(nc.scalar, w1_scales, 0)
+        nc.gpsimd.dma_start(gain[:, 0, :], gn.rearrange("(p t) o -> p (t o)", t=PACK))
+        nc.gpsimd.dma_start(w_raw[2][:], hbm_words(w3_words))
+        nc.gpsimd.dma_start(w_raw[1][:], hbm_words(w2_words))
+
+        plane_i = pick_plane[:].bitcast(I32)
+        nc.vector.memset(plane_i, 0)
+        for t in range(PACK):
+            nc.vector.memset(hwin[t][:, V:], 0.0)
+
+        nc.vector.tensor_copy(pick_s[:], xs[:].indirect(offs_t[:]))
+        pick_i = pick_s[:].bitcast(I32)
+        for i in range(2):
+            nc.scalar.dma_start(plane_i[2 + i : P : QUAD, :], pick_i[16 + i : P : QUAD, :])
+        for i in range(2, 4):
+            nc.sync.dma_start(xs_i[i:P:QUAD, :], xs_rows[i:16:4, :])
+        for q in range(4):
+            nc.vector.tensor_copy(plane_i[QUAD * q : QUAD * q + 2, :], pick_i[QUAD * q : QUAD * q + 2, :])
+
+        def deal(dst, src):
+            nc.vector.tensor_copy(
+                dst[:].rearrange("p (t m) -> p t m", t=PACK), src[:].rearrange("p (m t) -> p t m", t=PACK)
+            )
+
+        deal(w_deal[0], w_raw[0])
+        deal(w1s, ws_raw)
+        load_scale_rows(nc.sync, w3_scales, 4)
+        load_scale_rows(nc.sync, w2_scales, 8)
+
+        xw_u = xw[:].bitcast(U32)
+        y_ps = [ps.tile([P, S], F32, name="y_ps%d" % t) for t in range(PACK)]
+        for h in range(2):
+            cols = slice(h * HALF, (h + 1) * HALF)
+            nc.vector.tensor_copy(pick_w[:, cols], xw_u.indirect(offs_t[:, h * 16 : (h + 1) * 16]))
+            for t in range(PACK):
+                m = slice(t * P, (t + 1) * P)
+                nc.tensor.matmul_mx(
+                    out=y_ps[t][:, cols], lhsT=w_deal[0][:, m].bitcast(FP8X4), lhsT_scale=w1s[:, m],
+                    rhs=pick_w[:, cols].bitcast(FP8X4), rhs_scale=pick_plane[:, cols], start=True, stop=True,
+                )
+
+        nc.vector.tensor_copy(two_w[:], xw_u.indirect(two_t[:]))
+        nc.vector.tensor_copy(two_s[:], xs[:].indirect(two_t[:]))
+        deal(w_deal[2], w_raw[2])
+        deal(w_deal[1], w_raw[1])
+
+        sq = [sbt("sq%d" % t, [P, S], F32) for t in range(PACK)]
+        for t in range(PACK):
+            nc.scalar.activation(sq[t][:], y_ps[t][:], ACT.Square)
+
+        lined = [sbt("lined%d" % h, [P, PACK, HALF], F32) for h in range(2)]
+        ms = [sbt("ms%d" % h, [P, PACK, VH], F32) for h in range(2)]
+        root = [sbt("root%d" % h, [P, VH, PACK], F32) for h in range(2)]
+        zb = [sbt("zb%d" % h, [P, VH, PACK], BF16) for h in range(2)]
+        z_w = [sbt("z_w%d" % h, [P, VH], U32) for h in range(2)]
+        z_s = [sbt("z_s%d" % h, [P, VH], U8) for h in range(2)]
+
+        def line_up(h, t, on_vector):
+            window = sq[t][:].indirect(n1_t[:, h * 16 : (h + 1) * 16])
+            if on_vector:
+                nc.vector.tensor_copy(lined[h][:, t, :], window)
+            else:
+                nc.scalar.activation(lined[h][:, t, :], window, ACT.Copy)
+
+        def pair_sum(h, vs):
+            pairs = lined[h][:].rearrange("p t (v two) -> p t v two", two=2)
+            nc.vector.scalar_tensor_tensor(
+                ms[h][:, :, vs], pairs[:, :, vs, 0], 0.1, pairs[:, :, vs, 1], ALU.add, ALU.add
+            )
+
+        def take_root(h, vs):
+            nc.scalar.activation(root[h][:, vs, :], ms[h][:, :, vs].rearrange("p t v -> p v t"), ACT.Sqrt)
+
+        def apply_gain(h, vs):
+            n = vs.stop - vs.start
+            nc.vector.tensor_tensor(zb[h][:, vs, :], root[h][:, vs, :], gain[:].to_broadcast([P, n, PACK]), ALU.mult)
+
+        def quantize_z(h):
+            nc.vector.quantize_mx(
+                out=z_w[h][:].bitcast(FP8X4), scales=z_s[h][:], in_=zb[h][:].rearrange("p v t -> p (v t)")
+            )
+
+        h_ps = [ps.tile([P, V], F32, name="h_ps%d" % t) for t in range(PACK)]
+
+        def second_layer(h):
+            for t in range(PACK):
+                m = slice(t * P, (t + 1) * P)
+                nc.tensor.matmul_mx(
+                    out=h_ps[t][:, h * VH : (h + 1) * VH], lhsT=w_deal[1][:, m].bitcast(FP8X4),
+                    lhsT_scale=w23s[8:P, m], rhs=z_w[h][:].bitcast(FP8X4), rhs_scale=z_s[h][:],
+                    start=False, stop=(h == 1),
+                )
+
+        whole = slice(0, VH)
+        quarters = [slice(0, VH // 2), slice(VH // 2, VH)]
+        for t in range(PACK):
+            line_up(0, t, True)
+        line_up(1, 0, False)
+        line_up(1, 1, False)
+        pair_sum(0, whole)
+        take_root(0, whole)
+        line_up(1, 3, True)
+        line_up(1, 2, False)
+        deal(w23s, ws_raw)
+        for t in range(PACK):
+            m = slice(t * P, (t + 1) * P)
+            nc.tensor.matmul_mx(
+                out=h_ps[t][:], lhsT=w_deal[2][:, m].bitcast(FP8X4), lhsT_scale=w23s[4:P, m],
+                rhs=two_w[:].bitcast(FP8X4), rhs_scale=two_s[:], start=True, stop=False,
+            )
+        apply_gain(0, whole)
+        for vs in quarters:
+            pair_sum(1, vs)
+            take_root(1, vs)
+        quantize_z(0)
+        second_layer(0)
+        for vs in quarters:
+            apply_gain(1, vs)
+        quantize_z(1)
+        second_layer(1)
+
+        first = sbt("first", [P, PACK, V], F32)
+        other = sbt("other", [P, V], F32)
+        res = sbt("res", [P, PACK, V], F32)
+        out_rows = out_0.rearrange("(p t) v -> p t v", t=PACK)
+
+        nc.scalar.copy(hwin[0][:, :V], h_ps[0][:])
+        nc.vector.tensor_copy(hwin[1][:, :V], h_ps[1][:])
+        nc.vector.tensor_copy(hwin[2][:, :V], h_ps[2][:])
+        for t in range(PACK):
+            nc.scalar.activation(first[:, t, :], hwin[t][:].indirect(n2_t[:]), ACT.Copy)
+            if t == 0:
+                nc.scalar.copy(hwin[3][:, :V], h_ps[3][:])
+            if t < PACK - 1:
+                nc.vector.tensor_tensor(res[:, t, :], hwin[t][:].indirect(n3_t[:]), first[:, t, :], ALU.mult)
+            else:
+                nc.scalar.activation(other[:], hwin[t][:].indirect(n3_t[:]), ACT.Copy)
+                nc.vector.tensor_tensor(res[:, t, :], other[:], first[:, t, :], ALU.mult)
+            nc.sync.dma_start(out_rows[:, t, :], res[:, t, :])
+
+        resb = sbt("resb", [P, V, PACK], BF16)
+        o_w = sbt("o_w", [P, V], I32)
+        o_s = sbt("o_s", [P, V], U8)
+        cut = 160
+        nc.vector.tensor_copy(resb[:, :cut, :], res[:, :, :cut].rearrange("p t v -> p v t"))
+        nc.scalar.copy(resb[:, cut:, :], res[:, :, cut:].rearrange("p t v -> p v t"))
+        nc.vector.quantize_mx(out=o_w[:].bitcast(FP8X4), scales=o_s[:], in_=resb[:].rearrange("p v t -> p (v t)"))
+        nc.sync.dma_start(hbm_words(out_1), o_w[:])
+        os_i = o_s[:].bitcast(I32)
+        os_rows = out_2[0].bitcast(I32)
+        for q in range(4):
+            queue = nc.scalar if q % 2 == 0 else nc.sync
+            queue.dma_start(os_rows[4 * q : 4 * q + 4, :], os_i[QUAD * q : QUAD * q + 4, :])

@@ -20,7 +20,7 @@ PACK = 4
 QUAD = 32
 HALF = S // 2
 VH = V // 2
-SPARE = 16
+SPARE = 96
 
 
 def tile_picked_hmixhprmsprod_none_po_kernel(
@@ -35,10 +35,11 @@ def tile_picked_hmixhprmsprod_none_po_kernel(
     with ExitStack() as ctx:
         lists = ctx.enter_context(tc.tile_pool(name="lists", bufs=1))
         sb = ctx.enter_context(tc.tile_pool(name="sb", bufs=1))
+        shared = ctx.enter_context(tc.tile_pool(name="shared", bufs=1))
         ps = ctx.enter_context(tc.psum_pool(name="ps", bufs=1))
 
-        def sbt(name, shape, dtype):
-            return sb.tile(shape, dtype, name=name, align_bytes=64)
+        def sbt(name, shape, dtype, tag=""):
+            return sb.tile(shape, dtype, name=name, tag=tag or name, align_bytes=64)
 
         offs_t = lists.tile([P, S // 16], U16, name="offs_t")
         n1_t = lists.tile([P, S // 16], U16, name="n1_t")
@@ -46,87 +47,99 @@ def tile_picked_hmixhprmsprod_none_po_kernel(
         n2_t = lists.tile([P, V // 16], U16, name="n2_t")
         n3_t = lists.tile([P, V // 16], U16, name="n3_t")
 
-        xw = sbt("xw", [P, T], I32)
+        xw = shared.tile([P, T], I32, name="xw", offset=0, align_bytes=64)
         xs = sbt("xs", [P, T], U8)
-        w_raw = [sbt("w_raw%d" % i, [P, N], I32) for i in range(3)]
-        w_deal = [sbt("w_deal%d" % i, [P, N], I32) for i in range(3)]
-        ws_raw = sbt("ws_raw", [P, N], U8)
+        w1_raw = sbt("w1_raw", [P, N], I32)
+        w23_raw = sbt("w23_raw", [P, 2, N], I32)
+        w1_deal = sbt("w1_deal", [P, N], I32)
+        w1s_raw = sbt("w1s_raw", [P, N], U8)
         w1s = sbt("w1s", [P, N], U8)
-        w23s = sbt("w23s", [P, N], U8)
+        w23s_rows = sbt("w23s_rows", [16, 2 * N // 4], I32)
         gain = sbt("gain", [P, 1, PACK], F32)
         pick_w = sbt("pick_w", [P, S], U32)
         pick_s = sbt("pick_s", [P, S], U8)
         pick_plane = sbt("pick_plane", [P, S], U8)
-        two_w = sbt("two_w", [P, V], U32)
         two_s = sbt("two_s", [P, V], U8)
+        two_plane = sbt("two_plane", [P, V], U8)
         hwin = [sbt("hwin%d" % t, [P, V + SPARE], F32) for t in range(PACK)]
 
         xs_rows = x_scales[0].bitcast(I32)
         xs_i = xs[:].bitcast(I32)
+        w1s_i = w1s_raw[:].bitcast(I32)
 
-        nc.vector.memset(xs_i, 0)
-        nc.vector.memset(ws_raw[:].bitcast(I32), 0)
-        nc.gpsimd.dma_start(xw[:], hbm_words(x_words))
         nc.sync.dma_start(offs_t[:], offs)
-        nc.scalar.dma_start(xs_i[0:P:16, :], xs_rows[0:16:2, :])
-        nc.scalar.dma_start(xs_i[1:P:16, :], xs_rows[1:16:2, :])
+        nc.scalar.dma_start(xs_i, xs_rows.unsqueeze(1).to_broadcast([16, 8, T // 4]))
+        nc.sync.dma_start(w1_raw[:], hbm_words(w1_words))
         nc.sync.dma_start(two_t[:], two)
         nc.sync.dma_start(n1_t[:], n1)
         nc.sync.dma_start(n2_t[:], n2)
         nc.sync.dma_start(n3_t[:], n3)
-        nc.sync.dma_start(w_raw[0][:], hbm_words(w1_words))
-
-        def load_scale_rows(queue, scales, k):
-            rows = scales[0].bitcast(I32)
-            dst = ws_raw[:].bitcast(I32)
-            for q in range(4):
-                queue.dma_start(dst[QUAD * q + k : QUAD * q + k + 4, :], rows[4 * q : 4 * q + 4, :])
-
-        load_scale_rows(nc.scalar, w1_scales, 0)
+        nc.sync.dma_start(xw[:], hbm_words(x_words))
+        for w, scales in enumerate((w2_scales, w3_scales)):
+            nc.gpsimd.dma_start(w23s_rows[:, w * N // 4 : (w + 1) * N // 4], scales[0].bitcast(I32))
+        nc.gpsimd.dma_start(w23_raw[:, 1, :], hbm_words(w3_words))
+        nc.gpsimd.dma_start(w23_raw[:, 0, :], hbm_words(w2_words))
         nc.gpsimd.dma_start(gain[:, 0, :], gn.rearrange("(p t) o -> p (t o)", t=PACK))
-        nc.gpsimd.dma_start(w_raw[2][:], hbm_words(w3_words))
-        nc.gpsimd.dma_start(w_raw[1][:], hbm_words(w2_words))
 
-        plane_i = pick_plane[:].bitcast(I32)
-        nc.vector.memset(plane_i, 0)
-        for t in range(PACK):
+        nc.vector.memset(hwin[0][:, V:], 0.0)
+        warm = sbt("warm", [P, 1], F32)
+        nc.scalar.activation(warm[:], hwin[0][:, V : V + 1], ACT.Sqrt, bias=1.0)
+        nc.vector.memset(w1s_i, 0)
+        w1s_rows = w1_scales[0].bitcast(I32)
+        for q in range(4):
+            nc.scalar.dma_start(w1s_i[QUAD * q : QUAD * q + 4, :], w1s_rows[4 * q : 4 * q + 4, :])
+        for t in range(1, PACK):
             nc.vector.memset(hwin[t][:, V:], 0.0)
 
-        nc.vector.tensor_copy(pick_s[:], xs[:].indirect(offs_t[:]))
-        pick_i = pick_s[:].bitcast(I32)
-        for i in range(2):
-            nc.scalar.dma_start(plane_i[2 + i : P : QUAD, :], pick_i[16 + i : P : QUAD, :])
-        for i in range(2, 4):
-            nc.sync.dma_start(xs_i[i:P:QUAD, :], xs_rows[i:16:4, :])
-        for q in range(4):
-            nc.vector.tensor_copy(plane_i[QUAD * q : QUAD * q + 2, :], pick_i[QUAD * q : QUAD * q + 2, :])
+        def gather_plane(queue, plane, picked, offsets):
+            nc.vector.tensor_copy(picked[:], xs[:].indirect(offsets[:]))
+            plane_i, picked_i = plane[:].bitcast(I32), picked[:].bitcast(I32)
+            nc.vector.tensor_copy(plane_i, picked_i)
+            for i in range(1, 4):
+                queue.dma_start(plane_i[i:P:QUAD, :], picked_i[8 * i : P : QUAD, :])
 
         def deal(dst, src):
             nc.vector.tensor_copy(
-                dst[:].rearrange("p (t m) -> p t m", t=PACK), src[:].rearrange("p (m t) -> p t m", t=PACK)
+                dst.rearrange("p (w t m) -> p t w m", t=PACK, m=P), src.rearrange("p (w m t) -> p t w m", t=PACK, m=P)
             )
 
-        deal(w_deal[0], w_raw[0])
-        deal(w1s, ws_raw)
-        load_scale_rows(nc.sync, w3_scales, 4)
-        load_scale_rows(nc.sync, w2_scales, 8)
+        def deal_words(dst, src):
+            nc.vector.tensor_copy(
+                dst.rearrange("p (t m) -> p m t", t=PACK), src.rearrange("p (m t) -> p m t", t=PACK)
+            )
 
         xw_u = xw[:].bitcast(U32)
-        y_ps = [ps.tile([P, S], F32, name="y_ps%d" % t) for t in range(PACK)]
+        gather_plane(nc.sync, pick_plane, pick_s, offs_t)
+        gather_plane(nc.gpsimd, two_plane, two_s, two_t)
+        w23s_raw = sbt("w23s_raw", [P, 2 * N], U8, tag="xs")
+        w23s_i = w23s_raw[:].bitcast(I32)
+        nc.vector.memset(w23s_i, 0)
+        for q in range(4):
+            nc.sync.dma_start(w23s_i[QUAD * q : QUAD * q + 4, :], w23s_rows[4 * q : 4 * q + 4, :])
+        deal_words(w1_deal[:], w1_raw[:])
+        deal(w1s[:], w1s_raw[:])
+
+        y_ps = [ps.tile([P, S], F32, name="y_ps%d" % t, tag="y_ps%d" % t) for t in range(PACK)]
         for h in range(2):
             cols = slice(h * HALF, (h + 1) * HALF)
             nc.vector.tensor_copy(pick_w[:, cols], xw_u.indirect(offs_t[:, h * 16 : (h + 1) * 16]))
-            for t in range(PACK):
-                m = slice(t * P, (t + 1) * P)
+        for t in range(PACK):
+            m = slice(t * P, (t + 1) * P)
+            for h in range(2):
+                cols = slice(h * HALF, (h + 1) * HALF)
                 nc.tensor.matmul_mx(
-                    out=y_ps[t][:, cols], lhsT=w_deal[0][:, m].bitcast(FP8X4), lhsT_scale=w1s[:, m],
+                    out=y_ps[t][:, cols], lhsT=w1_deal[:, m].bitcast(FP8X4), lhsT_scale=w1s[:, m],
                     rhs=pick_w[:, cols].bitcast(FP8X4), rhs_scale=pick_plane[:, cols], start=True, stop=True,
                 )
 
+        two_w = sbt("two_w", [P, V], U32, tag="w1s_raw")
         nc.vector.tensor_copy(two_w[:], xw_u.indirect(two_t[:]))
-        nc.vector.tensor_copy(two_s[:], xs[:].indirect(two_t[:]))
-        deal(w_deal[2], w_raw[2])
-        deal(w_deal[1], w_raw[1])
+        w3_deal = shared.tile([P, N], I32, name="w3_deal", offset=0, align_bytes=64)
+        w2_deal = shared.tile([P, N], I32, name="w2_deal", offset=4 * N, align_bytes=64)
+        w23s = shared.tile([P, 2, N], U8, name="w23s", offset=8 * N, align_bytes=64)
+        deal_words(w3_deal[:], w23_raw[:, 1, :])
+        deal_words(w2_deal[:], w23_raw[:, 0, :])
+        deal(w23s[:].rearrange("p w n -> p (w n)"), w23s_raw[:])
 
         sq = [sbt("sq%d" % t, [P, S], F32) for t in range(PACK)]
         for t in range(PACK):
@@ -164,15 +177,18 @@ def tile_picked_hmixhprmsprod_none_po_kernel(
                 out=z_w[h][:].bitcast(FP8X4), scales=z_s[h][:], in_=zb[h][:].rearrange("p v t -> p (v t)")
             )
 
-        h_ps = [ps.tile([P, V], F32, name="h_ps%d" % t) for t in range(PACK)]
+        h_ps = [
+            [ps.tile([P, VH], F32, name="h_ps%d%d" % (h, t), tag=("y_ps%d", "h_ps%d")[h] % t) for t in range(PACK)]
+            for h in range(2)
+        ]
 
         def second_layer(h):
             for t in range(PACK):
                 m = slice(t * P, (t + 1) * P)
                 nc.tensor.matmul_mx(
-                    out=h_ps[t][:, h * VH : (h + 1) * VH], lhsT=w_deal[1][:, m].bitcast(FP8X4),
-                    lhsT_scale=w23s[8:P, m], rhs=z_w[h][:].bitcast(FP8X4), rhs_scale=z_s[h][:],
-                    start=False, stop=(h == 1),
+                    out=h_ps[h][t][:], lhsT=w2_deal[:, m].bitcast(FP8X4),
+                    lhsT_scale=w23s[:, 0, m], rhs=z_w[h][:].bitcast(FP8X4), rhs_scale=z_s[h][:],
+                    start=False, stop=True,
                 )
 
         whole = slice(0, VH)
@@ -185,13 +201,14 @@ def tile_picked_hmixhprmsprod_none_po_kernel(
         take_root(0, whole)
         line_up(1, 3, True)
         line_up(1, 2, False)
-        deal(w23s, ws_raw)
-        for t in range(PACK):
-            m = slice(t * P, (t + 1) * P)
-            nc.tensor.matmul_mx(
-                out=h_ps[t][:], lhsT=w_deal[2][:, m].bitcast(FP8X4), lhsT_scale=w23s[4:P, m],
-                rhs=two_w[:].bitcast(FP8X4), rhs_scale=two_s[:], start=True, stop=False,
-            )
+        for h in range(2):
+            cols = slice(h * VH, (h + 1) * VH)
+            for t in range(PACK):
+                m = slice(t * P, (t + 1) * P)
+                nc.tensor.matmul_mx(
+                    out=h_ps[h][t][:], lhsT=w3_deal[:, m].bitcast(FP8X4), lhsT_scale=w23s[:, 1, m],
+                    rhs=two_w[:, cols].bitcast(FP8X4), rhs_scale=two_plane[:, cols], start=True, stop=False,
+                )
         apply_gain(0, whole)
         for vs in quarters:
             pair_sum(1, vs)
@@ -200,6 +217,8 @@ def tile_picked_hmixhprmsprod_none_po_kernel(
         second_layer(0)
         for vs in quarters:
             apply_gain(1, vs)
+        for t in range(PACK):
+            nc.scalar.copy(hwin[t][:, :VH], h_ps[0][t][:])
         quantize_z(1)
         second_layer(1)
 
@@ -208,17 +227,26 @@ def tile_picked_hmixhprmsprod_none_po_kernel(
         res = sbt("res", [P, PACK, V], F32)
         out_rows = out_0.rearrange("(p t) v -> p t v", t=PACK)
 
-        nc.scalar.copy(hwin[0][:, :V], h_ps[0][:])
-        nc.vector.tensor_copy(hwin[1][:, :V], h_ps[1][:])
-        nc.vector.tensor_copy(hwin[2][:, :V], h_ps[2][:])
+        def fetch(t, on_vector):
+            window = hwin[t][:].indirect(n2_t[:])
+            if on_vector:
+                nc.vector.tensor_copy(first[:, t, :], window)
+            else:
+                nc.scalar.activation(first[:, t, :], window, ACT.Copy)
+
+        nc.scalar.copy(hwin[0][:, VH:V], h_ps[1][0][:])
+        nc.vector.tensor_copy(hwin[1][:, VH:V], h_ps[1][1][:])
+        fetch(0, False)
+        fetch(1, True)
+        nc.scalar.copy(hwin[2][:, VH:V], h_ps[1][2][:])
+        nc.scalar.copy(hwin[3][:, VH:V], h_ps[1][3][:])
+        fetch(2, False)
+        fetch(3, False)
+        nc.scalar.activation(other[:], hwin[3][:].indirect(n3_t[:]), ACT.Copy)
         for t in range(PACK):
-            nc.scalar.activation(first[:, t, :], hwin[t][:].indirect(n2_t[:]), ACT.Copy)
-            if t == 0:
-                nc.scalar.copy(hwin[3][:, :V], h_ps[3][:])
             if t < PACK - 1:
                 nc.vector.tensor_tensor(res[:, t, :], hwin[t][:].indirect(n3_t[:]), first[:, t, :], ALU.mult)
             else:
-                nc.scalar.activation(other[:], hwin[t][:].indirect(n3_t[:]), ACT.Copy)
                 nc.vector.tensor_tensor(res[:, t, :], other[:], first[:, t, :], ALU.mult)
             nc.sync.dma_start(out_rows[:, t, :], res[:, t, :])
 

@@ -54,45 +54,49 @@ def tile_picked_hmixhprmsprod_none_po_kernel(
         w1_deal = sbt("w1_deal", [P, N], I32)
         w1s_raw = sbt("w1s_raw", [P, N], U8)
         w1s = sbt("w1s", [P, N], U8)
-        w23s_rows = sbt("w23s_rows", [16, 2 * N // 4], I32)
+        w23s_raw = sbt("w23s_raw", [P, 2 * N], U8)
+        w23s = sbt("w23s", [P, 2 * N], U8)
+        two_plane = sbt("two_plane", [P, V], U8)
         gain = sbt("gain", [P, 1, PACK], F32)
         pick_w = sbt("pick_w", [P, S], U32)
         pick_s = sbt("pick_s", [P, S], U8)
         pick_plane = sbt("pick_plane", [P, S], U8)
         two_s = sbt("two_s", [P, V], U8)
-        two_plane = sbt("two_plane", [P, V], U8)
         hwin = [sbt("hwin%d" % t, [P, V + SPARE], F32) for t in range(PACK)]
 
         xs_rows = x_scales[0].bitcast(I32)
         xs_i = xs[:].bitcast(I32)
         w1s_i = w1s_raw[:].bitcast(I32)
 
+        def rows_by_eight(rows):
+            return rows.unsqueeze(1).to_broadcast([16, 8, rows.shape[1]])
+
+        nc.vector.memset(w1s_i, 0)
         nc.sync.dma_start(offs_t[:], offs)
-        nc.scalar.dma_start(xs_i, xs_rows.unsqueeze(1).to_broadcast([16, 8, T // 4]))
-        nc.sync.dma_start(w1_raw[:], hbm_words(w1_words))
-        nc.sync.dma_start(two_t[:], two)
+        nc.scalar.dma_start(xs_i, rows_by_eight(xs_rows))
+        nc.scalar.dma_start(w1_raw[:], hbm_words(w1_words))
+        nc.scalar.dma_start(xw[:], hbm_words(x_words))
+        w1s_rows = w1_scales[0].bitcast(I32)
+        for q in range(4):
+            nc.sync.dma_start(w1s_i[QUAD * q : QUAD * q + 4, :], w1s_rows[4 * q : 4 * q + 4, :])
         nc.sync.dma_start(n1_t[:], n1)
+        nc.sync.dma_start(two_t[:], two)
         nc.sync.dma_start(n2_t[:], n2)
         nc.sync.dma_start(n3_t[:], n3)
-        nc.sync.dma_start(xw[:], hbm_words(x_words))
         for w, scales in enumerate((w2_scales, w3_scales)):
-            nc.gpsimd.dma_start(w23s_rows[:, w * N // 4 : (w + 1) * N // 4], scales[0].bitcast(I32))
+            nc.gpsimd.dma_start(
+                w23s_raw[:].bitcast(I32)[:, w * N // 4 : (w + 1) * N // 4], rows_by_eight(scales[0].bitcast(I32))
+            )
         nc.gpsimd.dma_start(w23_raw[:, 1, :], hbm_words(w3_words))
         nc.gpsimd.dma_start(w23_raw[:, 0, :], hbm_words(w2_words))
         nc.gpsimd.dma_start(gain[:, 0, :], gn.rearrange("(p t) o -> p (t o)", t=PACK))
 
-        nc.vector.memset(hwin[0][:, V:], 0.0)
+        for t in range(PACK):
+            nc.vector.memset(hwin[t][:, V:], 0.0)
         warm = sbt("warm", [P, 1], F32)
         nc.scalar.activation(warm[:], hwin[0][:, V : V + 1], ACT.Sqrt, bias=1.0)
-        nc.vector.memset(w1s_i, 0)
-        w1s_rows = w1_scales[0].bitcast(I32)
-        for q in range(4):
-            nc.scalar.dma_start(w1s_i[QUAD * q : QUAD * q + 4, :], w1s_rows[4 * q : 4 * q + 4, :])
-        for t in range(1, PACK):
-            nc.vector.memset(hwin[t][:, V:], 0.0)
 
-        def gather_plane(queue, plane, picked, offsets):
-            nc.vector.tensor_copy(picked[:], xs[:].indirect(offsets[:]))
+        def place_rows(queue, plane, picked):
             plane_i, picked_i = plane[:].bitcast(I32), picked[:].bitcast(I32)
             nc.vector.tensor_copy(plane_i, picked_i)
             for i in range(1, 4):
@@ -109,37 +113,31 @@ def tile_picked_hmixhprmsprod_none_po_kernel(
             )
 
         xw_u = xw[:].bitcast(U32)
-        gather_plane(nc.sync, pick_plane, pick_s, offs_t)
-        gather_plane(nc.gpsimd, two_plane, two_s, two_t)
-        w23s_raw = sbt("w23s_raw", [P, 2 * N], U8, tag="xs")
-        w23s_i = w23s_raw[:].bitcast(I32)
-        nc.vector.memset(w23s_i, 0)
-        for q in range(4):
-            nc.sync.dma_start(w23s_i[QUAD * q : QUAD * q + 4, :], w23s_rows[4 * q : 4 * q + 4, :])
+        nc.vector.tensor_copy(pick_s[:], xs[:].indirect(offs_t[:]))
+        place_rows(nc.scalar, pick_plane, pick_s)
         deal_words(w1_deal[:], w1_raw[:])
         deal(w1s[:], w1s_raw[:])
 
         y_ps = [ps.tile([P, S], F32, name="y_ps%d" % t, tag="y_ps%d" % t) for t in range(PACK)]
-        for h in range(2):
-            cols = slice(h * HALF, (h + 1) * HALF)
-            nc.vector.tensor_copy(pick_w[:, cols], xw_u.indirect(offs_t[:, h * 16 : (h + 1) * 16]))
+        nc.vector.tensor_copy(pick_w[:], xw_u.indirect(offs_t[:]))
         for t in range(PACK):
             m = slice(t * P, (t + 1) * P)
-            for h in range(2):
-                cols = slice(h * HALF, (h + 1) * HALF)
-                nc.tensor.matmul_mx(
-                    out=y_ps[t][:, cols], lhsT=w1_deal[:, m].bitcast(FP8X4), lhsT_scale=w1s[:, m],
-                    rhs=pick_w[:, cols].bitcast(FP8X4), rhs_scale=pick_plane[:, cols], start=True, stop=True,
-                )
+            nc.tensor.matmul_mx(
+                out=y_ps[t][:], lhsT=w1_deal[:, m].bitcast(FP8X4), lhsT_scale=w1s[:, m],
+                rhs=pick_w[:].bitcast(FP8X4), rhs_scale=pick_plane[:], start=True, stop=True,
+            )
 
-        two_w = sbt("two_w", [P, V], U32, tag="w1s_raw")
+        two_w = sbt("two_w", [P, V], U32)
         nc.vector.tensor_copy(two_w[:], xw_u.indirect(two_t[:]))
+        nc.vector.tensor_copy(two_s[:], xs[:].indirect(two_t[:]))
+        place_rows(nc.sync, two_plane, two_s)
         w3_deal = shared.tile([P, N], I32, name="w3_deal", offset=0, align_bytes=64)
         w2_deal = shared.tile([P, N], I32, name="w2_deal", offset=4 * N, align_bytes=64)
-        w23s = shared.tile([P, 2, N], U8, name="w23s", offset=8 * N, align_bytes=64)
+        w23s_deal = shared.tile([P, 2 * N], U8, name="w23s_deal", offset=8 * N, align_bytes=64)
+        deal(w23s_deal[:], w23s_raw[:])
+        place_rows(nc.sync, w23s, w23s_deal)
         deal_words(w3_deal[:], w23_raw[:, 1, :])
         deal_words(w2_deal[:], w23_raw[:, 0, :])
-        deal(w23s[:].rearrange("p w n -> p (w n)"), w23s_raw[:])
 
         sq = [sbt("sq%d" % t, [P, S], F32) for t in range(PACK)]
         for t in range(PACK):
@@ -187,7 +185,7 @@ def tile_picked_hmixhprmsprod_none_po_kernel(
                 m = slice(t * P, (t + 1) * P)
                 nc.tensor.matmul_mx(
                     out=h_ps[h][t][:], lhsT=w2_deal[:, m].bitcast(FP8X4),
-                    lhsT_scale=w23s[:, 0, m], rhs=z_w[h][:].bitcast(FP8X4), rhs_scale=z_s[h][:],
+                    lhsT_scale=w23s[:, m], rhs=z_w[h][:].bitcast(FP8X4), rhs_scale=z_s[h][:],
                     start=False, stop=True,
                 )
 
@@ -206,7 +204,7 @@ def tile_picked_hmixhprmsprod_none_po_kernel(
             for t in range(PACK):
                 m = slice(t * P, (t + 1) * P)
                 nc.tensor.matmul_mx(
-                    out=h_ps[h][t][:], lhsT=w3_deal[:, m].bitcast(FP8X4), lhsT_scale=w23s[:, 1, m],
+                    out=h_ps[h][t][:], lhsT=w3_deal[:, m].bitcast(FP8X4), lhsT_scale=w23s[:, N + t * P : N + (t + 1) * P],
                     rhs=two_w[:, cols].bitcast(FP8X4), rhs_scale=two_plane[:, cols], start=True, stop=False,
                 )
         apply_gain(0, whole)

from contextlib import ExitStack

import concourse.mybir as mybir

K, T, S, V, N, H = 512, 2048, 512, 256, 512, 512
FLOPS = 2 * K * H * S + 2 * H * N * V + 2 * K * N * V

F32 = mybir.dt.float32
BF16 = mybir.dt.bfloat16
I32 = mybir.dt.int32
U32 = mybir.dt.uint32
U16 = mybir.dt.uint16
U8 = mybir.dt.uint8
FP8X4 = mybir.dt.float8_e4m3fn_x4
ACT = mybir.ActivationFunctionType
ALU = mybir.AluOpType

P = 128
PACK = 4
QUAD = 32
HALF = S // 2
VH = V // 2
SPARE = 96


def tile_picked_hmixhprmsprod_none_po_kernel(
    tc, x_words, x_scales, w1_words, w1_scales, gn, w2_words, w2_scales, w3_words, w3_scales,
    offs, n1, two, n2, n3, out_0, out_1, out_2,
):
    nc = tc.nc

    def hbm_words(words):
        return words[0].rearrange("p c r -> p (c r)").bitcast(I32)

    with ExitStack() as ctx:
        lists = ctx.enter_context(tc.tile_pool(name="lists", bufs=1))
        sb = ctx.enter_context(tc.tile_pool(name="sb", bufs=1))
        shared = ctx.enter_context(tc.tile_pool(name="shared", bufs=1))
        ps = ctx.enter_context(tc.psum_pool(name="ps", bufs=1))

        def sbt(name, shape, dtype, tag=""):
            return sb.tile(shape, dtype, name=name, tag=tag or name, align_bytes=64)

        offs_t = lists.tile([P, S // 16], U16, name="offs_t")
        n1_t = lists.tile([P, S // 16], U16, name="n1_t")
        two_t = lists.tile([P, V // 16], U16, name="two_t")
        n2_t = lists.tile([P, V // 16], U16, name="n2_t")
        n3_t = lists.tile([P, V // 16], U16, name="n3_t")

        xw = shared.tile([P, T], I32, name="xw", offset=0, align_bytes=64)
        xs = sbt("xs", [P, T], U8)
        w1_raw = sbt("w1_raw", [P, N], I32)
        w23_raw = sbt("w23_raw", [P, 2, N], I32)
        w1_deal = sbt("w1_deal", [P, N], I32)
        w1s_raw = sbt("w1s_raw", [P, N], U8)
        w1s = sbt("w1s", [P, N], U8)
        w23s_raw = sbt("w23s_raw", [P, 2 * N], U8)
        w23s = sbt("w23s", [P, 2 * N], U8)
        two_plane = sbt("two_plane", [P, V], U8)
        gain = sbt("gain", [P, 1, PACK], F32)
        pick_w = sbt("pick_w", [P, S], U32)
        pick_s = sbt("pick_s", [P, S], U8)
        pick_plane = sbt("pick_plane", [P, S], U8)
        two_s = sbt("two_s", [P, V], U8)
        hwin = [sbt("hwin%d" % t, [P, V + SPARE], F32) for t in range(PACK)]

        xs_rows = x_scales[0].bitcast(I32)
        xs_i = xs[:].bitcast(I32)
        w1s_i = w1s_raw[:].bitcast(I32)

        def rows_by_eight(rows):
            return rows.unsqueeze(1).to_broadcast([16, 8, rows.shape[1]])

        nc.vector.memset(w1s_i, 0)
        nc.sync.dma_start(offs_t[:], offs)
        nc.scalar.dma_start(xs_i, rows_by_eight(xs_rows))
        nc.scalar.dma_start(w1_raw[:], hbm_words(w1_words))
        nc.scalar.dma_start(xw[:], hbm_words(x_words))
        w1s_rows = w1_scales[0].bitcast(I32)
        for q in range(4):
            nc.sync.dma_start(w1s_i[QUAD * q : QUAD * q + 4, :], w1s_rows[4 * q : 4 * q + 4, :])
        nc.sync.dma_start(n1_t[:], n1)
        nc.sync.dma_start(two_t[:], two)
        nc.sync.dma_start(n2_t[:], n2)
        nc.sync.dma_start(n3_t[:], n3)
        for w, scales in enumerate((w2_scales, w3_scales)):
            nc.gpsimd.dma_start(
                w23s_raw[:].bitcast(I32)[:, w * N // 4 : (w + 1) * N // 4], rows_by_eight(scales[0].bitcast(I32))
            )
        nc.gpsimd.dma_start(w23_raw[:, 1, :], hbm_words(w3_words))
        nc.gpsimd.dma_start(w23_raw[:, 0, :], hbm_words(w2_words))
        nc.gpsimd.dma_start(gain[:, 0, :], gn.rearrange("(p t) o -> p (t o)", t=PACK))

        for t in range(PACK):
            nc.vector.memset(hwin[t][:, V:], 0.0)
        warm = sbt("warm", [P, 1], F32)
        nc.scalar.activation(warm[:], hwin[0][:, V : V + 1], ACT.Sqrt, bias=1.0)

        def place_rows(queue, plane, picked):
            plane_i, picked_i = plane[:].bitcast(I32), picked[:].bitcast(I32)
            nc.vector.tensor_copy(plane_i, picked_i)
            for i in range(1, 4):
                queue.dma_start(plane_i[i:P:QUAD, :], picked_i[8 * i : P : QUAD, :])

        def deal(dst, src):
            nc.vector.tensor_copy(
                dst.rearrange("p (w t m) -> p t w m", t=PACK, m=P), src.rearrange("p (w m t) -> p t w m", t=PACK, m=P)
            )

        def deal_words(dst, src):
            nc.vector.tensor_copy(
                dst.rearrange("p (t m) -> p m t", t=PACK), src.rearrange("p (m t) -> p m t", t=PACK)
            )

        xw_u = xw[:].bitcast(U32)
        nc.vector.tensor_copy(pick_s[:], xs[:].indirect(offs_t[:]))
        place_rows(nc.scalar, pick_plane, pick_s)
        deal_words(w1_deal[:], w1_raw[:])
        deal(w1s[:], w1s_raw[:])

        y_ps = [ps.tile([P, S], F32, name="y_ps%d" % t, tag="y_ps%d" % t) for t in range(PACK)]
        nc.vector.tensor_copy(pick_w[:], xw_u.indirect(offs_t[:]))
        for t in range(PACK):
            m = slice(t * P, (t + 1) * P)
            nc.tensor.matmul_mx(
                out=y_ps[t][:], lhsT=w1_deal[:, m].bitcast(FP8X4), lhsT_scale=w1s[:, m],
                rhs=pick_w[:].bitcast(FP8X4), rhs_scale=pick_plane[:], start=True, stop=True,
            )

        two_w = sbt("two_w", [P, V], U32)
        nc.vector.tensor_copy(two_w[:], xw_u.indirect(two_t[:]))
        nc.vector.tensor_copy(two_s[:], xs[:].indirect(two_t[:]))
        place_rows(nc.sync, two_plane, two_s)
        w3_deal = shared.tile([P, N], I32, name="w3_deal", offset=0, align_bytes=64)
        w2_deal = shared.tile([P, N], I32, name="w2_deal", offset=4 * N, align_bytes=64)
        w23s_deal = shared.tile([P, 2 * N], U8, name="w23s_deal", offset=8 * N, align_bytes=64)
        deal(w23s_deal[:], w23s_raw[:])
        place_rows(nc.sync, w23s, w23s_deal)
        deal_words(w3_deal[:], w23_raw[:, 1, :])
        deal_words(w2_deal[:], w23_raw[:, 0, :])

        sq = [sbt("sq%d" % t, [P, S], F32) for t in range(PACK)]
        for t in range(PACK):
            nc.scalar.activation(sq[t][:], y_ps[t][:], ACT.Square)

        lined = [sbt("lined%d" % h, [P, PACK, HALF], F32) for h in range(2)]
        ms = [sbt("ms%d" % h, [P, PACK, VH], F32) for h in range(2)]
        root = [sbt("root%d" % h, [P, VH, PACK], F32) for h in range(2)]
        zb = [sbt("zb%d" % h, [P, VH, PACK], BF16) for h in range(2)]
        z_w = [sbt("z_w%d" % h, [P, VH], U32) for h in range(2)]
        z_s = [sbt("z_s%d" % h, [P, VH], U8) for h in range(2)]

        def line_up(h, t, on_vector):
            window = sq[t][:].indirect(n1_t[:, h * 16 : (h + 1) * 16])
            if on_vector:
                nc.vector.tensor_copy(lined[h][:, t, :], window)
            else:
                nc.scalar.activation(lined[h][:, t, :], window, ACT.Copy)

        def pair_sum(h, vs):
            pairs = lined[h][:].rearrange("p t (v two) -> p t v two", two=2)
            nc.vector.scalar_tensor_tensor(
                ms[h][:, :, vs], pairs[:, :, vs, 0], 0.1, pairs[:, :, vs, 1], ALU.add, ALU.add
            )

        def take_root(h, vs):
            nc.scalar.activation(root[h][:, vs, :], ms[h][:, :, vs].rearrange("p t v -> p v t"), ACT.Sqrt)

        def apply_gain(h, vs):
            n = vs.stop - vs.start
            nc.vector.tensor_tensor(zb[h][:, vs, :], root[h][:, vs, :], gain[:].to_broadcast([P, n, PACK]), ALU.mult)

        def quantize_z(h):
            nc.vector.quantize_mx(
                out=z_w[h][:].bitcast(FP8X4), scales=z_s[h][:], in_=zb[h][:].rearrange("p v t -> p (v t)")
            )

        h_ps = [
            [ps.tile([P, VH], F32, name="h_ps%d%d" % (h, t), tag=("y_ps%d", "h_ps%d")[h] % t) for t in range(PACK)]
            for h in range(2)
        ]

        def second_layer(h):
            for t in range(PACK):
                m = slice(t * P, (t + 1) * P)
                nc.tensor.matmul_mx(
                    out=h_ps[h][t][:], lhsT=w2_deal[:, m].bitcast(FP8X4),
                    lhsT_scale=w23s[:, m], rhs=z_w[h][:].bitcast(FP8X4), rhs_scale=z_s[h][:],
                    start=False, stop=True,
                )

        whole = slice(0, VH)
        quarters = [slice(0, VH // 2), slice(VH // 2, VH)]
        for t in range(PACK):
            line_up(0, t, True)
        line_up(1, 0, False)
        line_up(1, 1, False)
        pair_sum(0, whole)
        take_root(0, whole)
        line_up(1, 3, True)
        line_up(1, 2, False)
        for h in range(2):
            cols = slice(h * VH, (h + 1) * VH)
            for t in range(PACK):
                m = slice(t * P, (t + 1) * P)
                nc.tensor.matmul_mx(
                    out=h_ps[h][t][:], lhsT=w3_deal[:, m].bitcast(FP8X4), lhsT_scale=w23s[:, N + t * P : N + (t + 1) * P],
                    rhs=two_w[:, cols].bitcast(FP8X4), rhs_scale=two_plane[:, cols], start=True, stop=False,
                )
        apply_gain(0, whole)
        for vs in quarters:
            pair_sum(1, vs)
            take_root(1, vs)
        quantize_z(0)
        second_layer(0)
        for vs in quarters:
            apply_gain(1, vs)
        for t in range(PACK):
            nc.scalar.copy(hwin[t][:, :VH], h_ps[0][t][:])
        quantize_z(1)
        second_layer(1)

        first = sbt("first", [P, PACK, V], F32)
        other = sbt("other", [P, V], F32)
        res = sbt("res", [P, PACK, V], F32)
        out_rows = out_0.rearrange("(p t) v -> p t v", t=PACK)

        def fetch(t, on_vector):
            window = hwin[t][:].indirect(n2_t[:])
            if on_vector:
                nc.vector.tensor_copy(first[:, t, :], window)
            else:
                nc.scalar.activation(first[:, t, :], window, ACT.Copy)

        nc.scalar.copy(hwin[0][:, VH:V], h_ps[1][0][:])
        nc.vector.tensor_copy(hwin[1][:, VH:V], h_ps[1][1][:])
        fetch(0, False)
        fetch(1, True)
        nc.scalar.copy(hwin[2][:, VH:V], h_ps[1][2][:])
        nc.scalar.copy(hwin[3][:, VH:V], h_ps[1][3][:])
        fetch(2, False)
        fetch(3, False)
        nc.scalar.activation(other[:], hwin[3][:].indirect(n3_t[:]), ACT.Copy)
        for t in range(PACK):
            if t < PACK - 1:
                nc.vector.tensor_tensor(res[:, t, :], hwin[t][:].indirect(n3_t[:]), first[:, t, :], ALU.mult)
            else:
                nc.vector.tensor_tensor(res[:, t, :], other[:], first[:, t, :], ALU.mult)
            nc.sync.dma_start(out_rows[:, t, :], res[:, t, :])

        resb = sbt("resb", [P, V, PACK], BF16)
        o_w = sbt("o_w", [P, V], I32)
        o_s = sbt("o_s", [P, V], U8)
        cut = 160
        nc.vector.tensor_copy(resb[:, :cut, :], res[:, :, :cut].rearrange("p t v -> p v t"))
        nc.scalar.copy(resb[:, cut:, :], res[:, :, cut:].rearrange("p t v -> p v t"))
        nc.vector.quantize_mx(out=o_w[:].bitcast(FP8X4), scales=o_s[:], in_=resb[:].rearrange("p v t -> p (v t)"))
        nc.sync.dma_start(hbm_words(out_1), o_w[:])
        os_i = o_s[:].bitcast(I32)
        os_rows = out_2[0].bitcast(I32)
        for q in range(4):
            queue = nc.scalar if q % 2 == 0 else nc.sync
            queue.dma_start(os_rows[4 * q : 4 * q + 4, :], os_i[QUAD * q : QUAD * q + 4, :])
